import numpy as np
import ml_dtypes

BF16 = ml_dtypes.bfloat16


def bf(x):
    return np.asarray(x, np.float32).astype(BF16)


def f32(x):
    return np.asarray(x, np.float32)


def f64(x):
    return np.asarray(x).astype(np.float64)


def striped(idx):
    return np.concatenate([l.reshape(-1, 16).T for l in idx])


def rows(idx, k):
    return np.tile(np.repeat(idx, 16, axis=0), (k // (16 * 8), 1))


def look(tab, idx):
    return np.take_along_axis(f64(tab), rows(idx, len(tab)), axis=1)


K, S, D, V, N, M = 256, 2048, 3, 512, 1536, 256


def setup_inputs():
    return {"tab": f32(np.random.standard_normal((K, S))), "x0": f32(1.0 * np.random.standard_normal((K, V))), "w": bf(np.random.standard_normal((K, M)) / np.sqrt(K)), "b": f32(0.5 * np.random.standard_normal((M, 1))), "offs": striped(np.stack([np.random.permutation(S)[:N] for _ in range(8)]))}


def reference(tab, x0, w, b, offs):
    idx = np.stack([g.T.reshape(-1) for g in np.split(offs, 8)])
    m = f64(x0)
    for d in range(D):
        m = np.maximum(m, look(tab, idx[:, d * V:(d + 1) * V]))
    x = m + np.log(np.exp(f64(x0) - m) + sum(np.exp(look(tab, idx[:, d * V:(d + 1) * V]) - m) for d in range(D)))
    return np.maximum(f64(w).T @ x + f64(b), 0.0)

@@ -1,0 +1,73 @@
+import concourse.mybir as mybir
+
+F32, BF16, U16 = mybir.dt.float32, mybir.dt.bfloat16, mybir.dt.uint16
+ALU = mybir.AluOpType
+ACT = mybir.ActivationFunctionType
+
+P = 128
+K, S, D, V, M = 256, 2048, 3, 512, 256
+BLOCKS = K // P
+FLOPS = 2 * K * M * V
+
+
+def tile_lookup_lse_relu_kernel(tc, tab, x0, w, b, offs, out):
+    nc = tc.nc
+    with (
+        tc.tile_pool(name="held", bufs=1) as held,
+        tc.tile_pool(name="work", bufs=2) as work,
+        tc.psum_pool(name="psum", bufs=1) as psum,
+    ):
+        offsets = held.tile([P, D * V // 16], U16, name="offsets")
+        nc.sync.dma_start(offsets[:], offs)
+        entries = [offsets[:, d * V // 16 : (d + 1) * V // 16] for d in range(D)]
+
+        node = [held.tile([P, V], F32, name=f"node{k}") for k in range(BLOCKS)]
+        table = [held.tile([P, S], F32, name=f"table{k}") for k in range(BLOCKS)]
+        weights = [held.tile([P, M], BF16, name=f"weights{k}") for k in range(BLOCKS)]
+        bias = [held.tile([P, 1], F32, name=f"bias{m}") for m in range(M // P)]
+        for k in range(BLOCKS):
+            nc.sync.dma_start(node[k][:], x0[k * P : (k + 1) * P, :])
+            nc.sync.dma_start(table[k][:], tab[k * P : (k + 1) * P, :])
+        for k in range(BLOCKS):
+            nc.sync.dma_start(weights[k][:], w[k * P : (k + 1) * P, :])
+        for m in range(M // P):
+            nc.sync.dma_start(bias[m][:], b[m * P : (m + 1) * P, :])
+
+        x = [held.tile([P, V], BF16, name=f"x{k}") for k in range(BLOCKS)]
+        for k in range(BLOCKS):
+            h = node[k]
+            for d in range(D):
+                larger = work.tile([P, V], F32, name=f"larger{d}")
+                nc.vector.tensor_tensor(larger[:], table[k][:].indirect(entries[d]), h[:], ALU.max)
+                h = larger
+
+            below = work.tile([P, V], F32, name="below_node")
+            nc.vector.tensor_tensor(below[:], node[k][:], h[:], ALU.subtract)
+            total = work.tile([P, V], F32, name="exp_node")
+            nc.scalar.activation(total[:], below[:], ACT.Exp)
+            for d in range(D):
+                below = work.tile([P, V], F32, name=f"below{d}")
+                nc.vector.tensor_tensor(below[:], table[k][:].indirect(entries[d]), h[:], ALU.subtract)
+                term = work.tile([P, V], F32, name=f"exp{d}")
+                nc.scalar.activation(term[:], below[:], ACT.Exp)
+                longer = work.tile([P, V], F32, name=f"total{d}")
+                nc.vector.tensor_tensor(longer[:], total[:], term[:], ALU.add)
+                total = longer
+
+            log_total = work.tile([P, V], F32, name="log_total")
+            nc.scalar.activation(log_total[:], total[:], ACT.Ln)
+            nc.vector.tensor_tensor(x[k][:], log_total[:], h[:], ALU.add)
+
+        for m in range(M // P):
+            product = psum.tile([P, V], F32, name=f"product{m}")
+            for k in range(BLOCKS):
+                nc.tensor.matmul(
+                    product[:],
+                    weights[k][:, m * P : (m + 1) * P],
+                    x[k][:],
+                    start=k == 0,
+                    stop=k == BLOCKS - 1,
+                )
+            result = work.tile([P, V], F32, name=f"result{m}")
+            nc.scalar.activation(result[:], product[:], ACT.Relu, bias=bias[m][:])
+            nc.sync.dma_start(out[m * P : (m + 1) * P, :], result[:])

@@ -1,4 +1,5 @@
 import concourse.mybir as mybir
+from concourse.masks import make_identity
 
 F32, BF16, U16 = mybir.dt.float32, mybir.dt.bfloat16, mybir.dt.uint16
 ALU = mybir.AluOpType
@@ -26,48 +27,68 @@ def tile_lookup_lse_relu_kernel(tc, tab, x0, w, b, offs, out):
         weights = [held.tile([P, M], BF16, name=f"weights{k}") for k in range(BLOCKS)]
         bias = [held.tile([P, 1], F32, name=f"bias{m}") for m in range(M // P)]
         for k in range(BLOCKS):
-            nc.sync.dma_start(node[k][:], x0[k * P : (k + 1) * P, :])
-            nc.sync.dma_start(table[k][:], tab[k * P : (k + 1) * P, :])
+            rows = slice(k * P, (k + 1) * P)
+            nc.sync.dma_start(node[k][:], x0[rows, :])
+            nc.sync.dma_start(table[k][:], tab[rows, :])
         for k in range(BLOCKS):
             nc.sync.dma_start(weights[k][:], w[k * P : (k + 1) * P, :])
         for m in range(M // P):
             nc.sync.dma_start(bias[m][:], b[m * P : (m + 1) * P, :])
 
-        x = [held.tile([P, V], BF16, name=f"x{k}") for k in range(BLOCKS)]
+        identity = held.tile([P, P], F32, name="identity")
+        make_identity(nc, identity[:])
+
+        largest = list(node)
+        total = [psum.tile([P, V], F32, name=f"total{k}") for k in range(BLOCKS)]
+
+        def raise_maximum(k, d):
+            larger = held.tile([P, V], F32, name=f"larger{k}_{d}")
+            nc.vector.tensor_tensor(larger[:], table[k][:].indirect(entries[d]), largest[k][:], ALU.max)
+            largest[k] = larger
+
+        def add_exponential(k, term):
+            value = node[k][:] if term == 0 else table[k][:].indirect(entries[term - 1])
+            below = work.tile([P, V], F32, name=f"below{term}")
+            nc.vector.tensor_tensor(below[:], value, largest[k][:], ALU.subtract)
+            exponential = work.tile([P, V], F32, name=f"exponential{term}")
+            nc.scalar.activation(exponential[:], below[:], ACT.Exp)
+            nc.tensor.matmul(total[k][:], identity[:], exponential[:], start=term == 0, stop=term == D)
+
+        for k in range(BLOCKS + 1):
+            for step in range(D + 1):
+                if k < BLOCKS and step < D:
+                    raise_maximum(k, step)
+                if k > 0:
+                    add_exponential(k - 1, step)
+
+        halves = [slice(0, V // 2), slice(V // 2, V)]
+        products = {
+            (m, c): psum.tile([P, V // 2], F32, name=f"product{m}_{c}") for c in range(2) for m in range(M // P)
+        }
+
+        log_total = [held.tile([P, V], F32, name=f"log_total{k}") for k in range(BLOCKS)]
         for k in range(BLOCKS):
-            h = node[k]
-            for d in range(D):
-                larger = work.tile([P, V], F32, name=f"larger{d}")
-                nc.vector.tensor_tensor(larger[:], table[k][:].indirect(entries[d]), h[:], ALU.max)
-                h = larger
+            for half in halves:
+                nc.scalar.activation(log_total[k][:, half], total[k][:, half], ACT.Ln)
 
-            below = work.tile([P, V], F32, name="below_node")
-            nc.vector.tensor_tensor(below[:], node[k][:], h[:], ALU.subtract)
-            total = work.tile([P, V], F32, name="exp_node")
-            nc.scalar.activation(total[:], below[:], ACT.Exp)
-            for d in range(D):
-                below = work.tile([P, V], F32, name=f"below{d}")
-                nc.vector.tensor_tensor(below[:], table[k][:].indirect(entries[d]), h[:], ALU.subtract)
-                term = work.tile([P, V], F32, name=f"exp{d}")
-                nc.scalar.activation(term[:], below[:], ACT.Exp)
-                longer = work.tile([P, V], F32, name=f"total{d}")
-                nc.vector.tensor_tensor(longer[:], total[:], term[:], ALU.add)
-                total = longer
+        for k in range(BLOCKS):
+            for c, half in enumerate(halves):
+                x = work.tile([P, V // 2], BF16, name=f"x{c}")
+                nc.vector.tensor_tensor(x[:], log_total[k][:, half], largest[k][:, half], ALU.add)
+                for m in range(M // P):
+                    nc.tensor.matmul(
+                        products[m, c][:],
+                        weights[k][:, m * P : (m + 1) * P],
+                        x[:],
+                        start=k == 0,
+                        stop=k == BLOCKS - 1,
+                    )
 
-            log_total = work.tile([P, V], F32, name="log_total")
-            nc.scalar.activation(log_total[:], total[:], ACT.Ln)
-            nc.vector.tensor_tensor(x[k][:], log_total[:], h[:], ALU.add)
-
-        for m in range(M // P):
-            product = psum.tile([P, V], F32, name=f"product{m}")
-            for k in range(BLOCKS):
-                nc.tensor.matmul(
-                    product[:],
-                    weights[k][:, m * P : (m + 1) * P],
-                    x[k][:],
-                    start=k == 0,
-                    stop=k == BLOCKS - 1,
-                )
-            result = work.tile([P, V], F32, name=f"result{m}")
-            nc.scalar.activation(result[:], product[:], ACT.Relu, bias=bias[m][:])
-            nc.sync.dma_start(out[m * P : (m + 1) * P, :], result[:])
+        for c, half in enumerate(halves):
+            for m in range(M // P):
+                result = work.tile([P, V // 2], F32, name=f"result{m}_{c}")
+                if m % 2 == 0:
+                    nc.scalar.activation(result[:], products[m, c][:], ACT.Relu, bias=bias[m][:])
+                else:
+                    nc.vector.tensor_scalar(result[:], products[m, c][:], bias[m][:], 0.0, ALU.add, ALU.max)
+                nc.sync.dma_start(out[m * P : (m + 1) * P, half], result[:])

@@ -26,7 +26,9 @@ def tile_lookup_lse_relu_kernel(tc, tab, x0, w, b, offs, out):
         table = [held.tile([P, S], F32, name=f"table{k}") for k in range(BLOCKS)]
         weights = [held.tile([P, M], BF16, name=f"weights{k}") for k in range(BLOCKS)]
         bias = [held.tile([P, 1], F32, name=f"bias{m}") for m in range(M // P)]
-        for k in range(BLOCKS):
+        nc.scalar.dma_start(node[0][:], x0[:P, :])
+        nc.sync.dma_start(table[0][:], tab[:P, :])
+        for k in range(1, BLOCKS):
             rows = slice(k * P, (k + 1) * P)
             nc.sync.dma_start(node[k][:], x0[rows, :])
             nc.sync.dma_start(table[k][:], tab[rows, :])

import concourse.mybir as mybir
from concourse.masks import make_identity

F32, BF16, U16 = mybir.dt.float32, mybir.dt.bfloat16, mybir.dt.uint16
ALU = mybir.AluOpType
ACT = mybir.ActivationFunctionType

P = 128
K, S, D, V, M = 256, 2048, 3, 512, 256
BLOCKS = K // P
FLOPS = 2 * K * M * V


def tile_lookup_lse_relu_kernel(tc, tab, x0, w, b, offs, out):
    nc = tc.nc
    with (
        tc.tile_pool(name="held", bufs=1) as held,
        tc.tile_pool(name="work", bufs=2) as work,
        tc.psum_pool(name="psum", bufs=1) as psum,
    ):
        offsets = held.tile([P, D * V // 16], U16, name="offsets")
        nc.sync.dma_start(offsets[:], offs)
        entries = [offsets[:, d * V // 16 : (d + 1) * V // 16] for d in range(D)]

        node = [held.tile([P, V], F32, name=f"node{k}") for k in range(BLOCKS)]
        table = [held.tile([P, S], F32, name=f"table{k}") for k in range(BLOCKS)]
        weights = [held.tile([P, M], BF16, name=f"weights{k}") for k in range(BLOCKS)]
        bias = [held.tile([P, 1], F32, name=f"bias{m}") for m in range(M // P)]
        nc.scalar.dma_start(node[0][:], x0[:P, :])
        nc.sync.dma_start(table[0][:], tab[:P, :])
        for k in range(1, BLOCKS):
            rows = slice(k * P, (k + 1) * P)
            nc.sync.dma_start(node[k][:], x0[rows, :])
            nc.sync.dma_start(table[k][:], tab[rows, :])
        for k in range(BLOCKS):
            nc.sync.dma_start(weights[k][:], w[k * P : (k + 1) * P, :])
        for m in range(M // P):
            nc.sync.dma_start(bias[m][:], b[m * P : (m + 1) * P, :])

        identity = held.tile([P, P], F32, name="identity")
        make_identity(nc, identity[:])

        largest = list(node)
        total = [psum.tile([P, V], F32, name=f"total{k}") for k in range(BLOCKS)]

        def raise_maximum(k, d):
            larger = held.tile([P, V], F32, name=f"larger{k}_{d}")
            nc.vector.tensor_tensor(larger[:], table[k][:].indirect(entries[d]), largest[k][:], ALU.max)
            largest[k] = larger

        def add_exponential(k, term):
            value = node[k][:] if term == 0 else table[k][:].indirect(entries[term - 1])
            below = work.tile([P, V], F32, name=f"below{term}")
            nc.vector.tensor_tensor(below[:], value, largest[k][:], ALU.subtract)
            exponential = work.tile([P, V], F32, name=f"exponential{term}")
            nc.scalar.activation(exponential[:], below[:], ACT.Exp)
            nc.tensor.matmul(total[k][:], identity[:], exponential[:], start=term == 0, stop=term == D)

        for k in range(BLOCKS + 1):
            for step in range(D + 1):
                if k < BLOCKS and step < D:
                    raise_maximum(k, step)
                if k > 0:
                    add_exponential(k - 1, step)

        halves = [slice(0, V // 2), slice(V // 2, V)]
        products = {
            (m, c): psum.tile([P, V // 2], F32, name=f"product{m}_{c}") for c in range(2) for m in range(M // P)
        }

        log_total = [held.tile([P, V], F32, name=f"log_total{k}") for k in range(BLOCKS)]
        for k in range(BLOCKS):
            for half in halves:
                nc.scalar.activation(log_total[k][:, half], total[k][:, half], ACT.Ln)

        for k in range(BLOCKS):
            for c, half in enumerate(halves):
                x = work.tile([P, V // 2], BF16, name=f"x{c}")
                nc.vector.tensor_tensor(x[:], log_total[k][:, half], largest[k][:, half], ALU.add)
                for m in range(M // P):
                    nc.tensor.matmul(
                        products[m, c][:],
                        weights[k][:, m * P : (m + 1) * P],
                        x[:],
                        start=k == 0,
                        stop=k == BLOCKS - 1,
                    )

        for c, half in enumerate(halves):
            for m in range(M // P):
                result = work.tile([P, V // 2], F32, name=f"result{m}_{c}")
                if m % 2 == 0:
                    nc.scalar.activation(result[:], products[m, c][:], ACT.Relu, bias=bias[m][:])
                else:
                    nc.vector.tensor_scalar(result[:], products[m, c][:], bias[m][:], 0.0, ALU.add, ALU.max)
                nc.sync.dma_start(out[m * P : (m + 1) * P, half], result[:])
